import numpy as np
import ml_dtypes


def mxq(x, axis, fmt="e4m3"):
    dtype, down = {"e4m3": (ml_dtypes.float8_e4m3fn, 7), "e5m2": (ml_dtypes.float8_e5m2, 14)}[fmt]
    v = np.moveaxis(np.asarray(x, np.float32).astype(ml_dtypes.bfloat16).astype(np.float64), axis, -1)
    blocks = v.reshape(v.shape[:-1] + (-1, 32))
    amax = np.abs(blocks).max(-1, keepdims=True)
    byte = np.maximum(np.where(amax > 0, np.frexp(amax)[1] - 1 + 127, 0) - down, 1)
    scale = np.exp2(byte - 127.0)
    codes = (blocks / scale).astype(np.float32).astype(dtype).astype(np.float64)
    return np.moveaxis((codes * scale).reshape(v.shape), -1, axis)


WIDE = False


def mx_kscale(k):
    if not WIDE:
        return np.ones(k)
    levels = np.array([10, -10, 5, -5, 0])
    if k % 512:
        return np.exp2(np.random.permutation(np.resize(levels, k // 32))).repeat(32)
    a = np.empty((k // 512, 16))
    for p in range(k // 512):
        a[p, :8] = np.random.permutation(np.resize(levels, 8))
        for g in range(8):
            far = levels[np.abs(levels - a[p, g]) >= 10]
            a[p, g + 8] = far[np.random.randint(len(far))]
    return np.exp2(a.ravel()).repeat(32)


def f64(x):
    return np.asarray(x).astype(np.float64)


def striped8(idx):
    return np.concatenate([v.reshape(-1, 16).T for v in idx]).astype(np.uint16)


def unstriped8(offs):
    return np.stack([offs[16 * g:16 * g + 16].T.reshape(-1) for g in range(8)]).astype(np.int64)


E2M1 = np.array([0.0, 0.5, 1.0, 1.5, 2.0, 3.0, 4.0, 6.0, -0.0, -0.5, -1.0, -1.5, -2.0, -3.0, -4.0, -6.0])


def pack_weight(w, fmt):
    k, n = w.shape
    w = f64(np.asarray(w, np.float32).astype(ml_dtypes.bfloat16)).reshape(k // 32, 32, n)
    amax = np.abs(w).max(1)
    if fmt == "e4m3":
        byte = np.frexp(amax)[1] - 1 + 127 - 7
    else:
        mant, ex = np.frexp(amax / 6.0)
        byte = np.where(mant > 0.5, ex, ex - 1) + 127
    byte = np.clip(np.where(amax > 0, byte, 1), 1, 254)
    scaled = (w * np.exp2(127.0 - byte)[:, None, :]).reshape(k, n).astype(np.float32)
    by_word = np.ascontiguousarray(scaled.reshape(k // 512, 128, 4, n).transpose(0, 1, 3, 2))
    if fmt == "e4m3":
        words = by_word.astype(ml_dtypes.float8_e4m3fn).view(np.uint8)
    else:
        c = by_word.astype(ml_dtypes.float4_e2m1fn).view(np.uint8) & 0xF
        words = (c[..., 0::2] | (c[..., 1::2] << 4)).reshape(k // 512, 128, 2 * n)
    return np.ascontiguousarray(words), np.ascontiguousarray(byte.astype(np.uint8).reshape(k // 512, 16, n))


def unpack_weight(words, scales, fmt):
    g, _, n = scales.shape
    words = np.ascontiguousarray(words).reshape(g, 128, n, -1)
    if fmt == "e4m3":
        vals = words.view(ml_dtypes.float8_e4m3fn).astype(np.float64)
    else:
        nib = np.empty((g, 128, n, 4), np.uint8)
        nib[..., 0::2] = words & 0xF
        nib[..., 1::2] = words >> 4
        vals = E2M1[nib]
    vals = vals * np.repeat(np.exp2(scales.astype(np.float64) - 127.0), 8, axis=1)[..., None]
    return vals.transpose(0, 1, 3, 2).reshape(g * 512, n)


K, M, T, S = 1536, 128, 1024, 512


def setup_inputs():
    n = np.random.standard_normal
    s = mx_kscale(K)[:, None]
    w = n((K, M)) / np.sqrt(K) / s
    w4 = pack_weight(w, "e2m1")
    rest = w - unpack_weight(*w4, "e2m1")
    p_r8 = pack_weight(rest, "e4m3")
    return {
        "xT": (n((K, T)) * s).astype(np.float32),
        "w4_words": w4[0],
        "w4_scales": w4[1],
        "r8_words": p_r8[0],
        "r8_scales": p_r8[1],
        "wgt": np.repeat(np.random.uniform(0.5, 2.0, (8, S)), 16, axis=0).astype(np.float32),
        "wgo": np.repeat(np.random.uniform(0.5, 2.0, (8, S)), 16, axis=0).astype(np.float32),
        "offs": striped8(np.stack([np.random.permutation(T)[:S] for _ in range(8)])),
        "offs2": striped8(np.stack([np.random.permutation(T)[:S] for _ in range(8)])),
    }


def reference(xT, w4_words, w4_scales, r8_words, r8_scales, wgt, wgo, offs, offs2):
    idx = unstriped8(offs)
    group = np.arange(K) % 512 // 64
    xg = f64(wgt)[np.arange(K) // 4 % 128] * f64(xT)[np.arange(K)[:, None], idx[group]]
    xT_ = mxq(xg, 0, "e4m3")
    w4_ = unpack_weight(w4_words, w4_scales, "e2m1")
    r8_ = unpack_weight(r8_words, r8_scales, "e4m3")
    y = w4_.T @ xT_ + r8_.T @ xT_
    place = unstriped8(offs2)[np.arange(M) % 128 // 16]
    out = np.zeros((M, T))
    out[np.arange(M)[:, None], place] = f64(wgo)[np.arange(M) % 128] * (y)
    return out

@@ -1,0 +1,183 @@
+from contextlib import ExitStack
+
+import concourse.mybir as mybir
+
+K, M, T, S = 1536, 128, 1024, 512
+FLOPS = 2 * 2 * K * M * S
+
+P = 128
+PACK = 4
+PASSES = K // (P * PACK)
+HALF = S // 2
+QUARTER = S // 4
+LANES = 16
+
+F32 = mybir.dt.float32
+BF16 = mybir.dt.bfloat16
+I32 = mybir.dt.int32
+U32 = mybir.dt.uint32
+U16 = mybir.dt.uint16
+U8 = mybir.dt.uint8
+FP8X4 = mybir.dt.float8_e4m3fn_x4
+FP4X4 = mybir.dt.float4_e2m1fn_x4
+MULT = mybir.AluOpType.mult
+
+
+def tile_list_hboth_none_kernel(
+    tc, xT, w4_words, w4_scales, r8_words, r8_scales, wgt, wgo, offs, offs2, out
+):
+    nc = tc.nc
+    with ExitStack() as ctx:
+        lists = ctx.enter_context(tc.tile_pool(name="lists", bufs=1))
+        keep = ctx.enter_context(tc.tile_pool(name="keep", bufs=1))
+        psum = ctx.enter_context(tc.psum_pool(name="psum", bufs=1))
+
+        gather_list = lists.tile([P, S // LANES], U16, name="gather_list")
+        scatter_list = lists.tile([P, S // LANES], U16, name="scatter_list")
+
+        planes = xT.rearrange("(a p i) t -> a i p t", a=PASSES, i=PACK)
+        x = [
+            [keep.tile([P, T], F32, name=f"x{a}_{i}") for i in range(PACK)]
+            for a in range(PASSES)
+        ]
+        wgt_sb = [keep.tile([P, HALF], F32, name=f"wgt{h}") for h in range(2)]
+        wgo_sb = keep.tile([P, S], F32, name="wgo_sb")
+        w4 = keep.tile([P, PASSES, 2 * M], U8, name="w4", align_bytes=64)
+        r8 = keep.tile([P, PASSES, PACK * M], U8, name="r8", align_bytes=64)
+        w4_s = keep.tile([P, PASSES, M], U8, name="w4_s", align_bytes=64)
+        r8_s = keep.tile([P, PASSES, M], U8, name="r8_s", align_bytes=64)
+        placed = keep.tile([P, T], F32, name="placed")
+
+        nc.sync.dma_start(gather_list[:], offs)
+        nc.sync.dma_start(x[0][0][:], planes[0, 0])
+        nc.sync.dma_start(wgt_sb[0][:], wgt[:, 0:HALF])
+        nc.sync.dma_start(wgt_sb[1][:], wgt[:, HALF:S])
+        for i in range(1, PACK):
+            nc.sync.dma_start(x[0][i][:], planes[0, i])
+        nc.sync.dma_start(x[1][0][:], planes[1, 0])
+        nc.sync.dma_start(w4[:].bitcast(I32), w4_words.rearrange("a p b -> p a b").bitcast(I32))
+        nc.sync.dma_start(r8[:].bitcast(I32), r8_words.rearrange("a p n i -> p a (n i)").bitcast(I32))
+        for i in range(1, PACK):
+            nc.sync.dma_start(x[1][i][:], planes[1, i])
+        for i in range(PACK):
+            nc.sync.dma_start(x[2][i][:], planes[2, i])
+        nc.sync.dma_start(scatter_list[:], offs2)
+        nc.sync.dma_start(wgo_sb[:], wgo)
+
+        nc.vector.memset(w4_s[:].rearrange("p a n -> p (a n)").bitcast(I32), 0)
+        nc.vector.memset(r8_s[:].rearrange("p a n -> p (a n)").bitcast(I32), 0)
+        nc.vector.memset(placed[:], 0.0)
+        for scales, rows in ((w4_s, w4_scales), (r8_s, r8_scales)):
+            for q in range(4):
+                nc.gpsimd.dma_start(
+                    scales[32 * q : 32 * q + 4].bitcast(I32),
+                    rows[:, 4 * q : 4 * q + 4, :].rearrange("a r n -> r a n").bitcast(I32),
+                )
+
+        sums = [psum.tile([P, QUARTER], F32, name=f"sum{q}") for q in range(4)]
+        y = [keep.tile([P, HALF], F32, name=f"y{h}") for h in range(2)]
+
+        chunks = [
+            [(0, HALF), (HALF, HALF)],
+            [(0, HALF), (HALF, HALF)],
+            [(0, HALF), (HALF, QUARTER), (HALF + QUARTER, QUARTER)],
+        ]
+        state = {}
+        for a in range(PASSES):
+            for j0, n in chunks[a]:
+                state[a, j0] = (
+                    n,
+                    keep.tile([P, PACK, n], F32, name=f"g{a}_{j0}"),
+                    keep.tile([P, n, PACK], BF16, name=f"b{a}_{j0}", align_bytes=64),
+                    keep.tile([P, n], U32, name=f"c{a}_{j0}", align_bytes=64),
+                    keep.tile([P, n], U8, name=f"s{a}_{j0}", align_bytes=64),
+                )
+
+        def gather(a, i, j0):
+            n, g = state[a, j0][0:2]
+            w0 = j0 % HALF
+            nc.vector.tensor_tensor(
+                g[:, i, :],
+                x[a][i][:].indirect(gather_list[:, j0 // LANES : (j0 + n) // LANES]),
+                wgt_sb[j0 // HALF][:, w0 : w0 + n],
+                MULT,
+            )
+
+        def interleave(a, j0):
+            n, g, b = state[a, j0][0:3]
+            nc.scalar.copy(b[:], g[:].rearrange("p i c -> p c i"))
+
+        def quantize(a, j0):
+            n, g, b, c, s = state[a, j0]
+            nc.vector.quantize_mx(
+                out=c[:].bitcast(FP8X4), scales=s[:], in_=b[:].rearrange("p c i -> p (c i)")
+            )
+            for k0 in range(0, n, QUARTER):
+                cols = slice(k0, k0 + QUARTER)
+                acc = sums[(j0 + k0) // QUARTER]
+                nc.tensor.matmul_mx(
+                    out=acc[:],
+                    lhsT=w4[:, a, :].bitcast(FP4X4),
+                    lhsT_scale=w4_s[:, a, :],
+                    rhs=c[:, cols].bitcast(FP8X4),
+                    rhs_scale=s[:, cols],
+                    start=(a == 0),
+                    stop=False,
+                )
+                nc.tensor.matmul_mx(
+                    out=acc[:],
+                    lhsT=r8[:, a, :].bitcast(FP8X4),
+                    lhsT_scale=r8_s[:, a, :],
+                    rhs=c[:, cols].bitcast(FP8X4),
+                    rhs_scale=s[:, cols],
+                    start=False,
+                    stop=(a == PASSES - 1),
+                )
+
+        def drain(q):
+            c0 = (q % 2) * QUARTER
+            nc.scalar.copy(y[q // 2][:, c0 : c0 + QUARTER], sums[q][:])
+
+        def scatter(h):
+            nc.vector.tensor_tensor(
+                placed[:].indirect(scatter_list[:, h * HALF // LANES : (h + 1) * HALF // LANES]),
+                y[h][:],
+                wgo_sb[:, h * HALF : (h + 1) * HALF],
+                MULT,
+            )
+
+        for a in range(2):
+            for i in range(PACK):
+                gather(a, i, 0)
+                if i == PACK - 1:
+                    interleave(a, 0)
+                gather(a, i, HALF)
+                if i == PACK - 1:
+                    interleave(a, HALF)
+                if a == 1 and i == 1:
+                    quantize(0, 0)
+                if a == 1 and i == 2:
+                    quantize(0, HALF)
+        for i in range(PACK):
+            gather(2, i, 0)
+            if i == 1:
+                quantize(1, 0)
+            if i == 2:
+                quantize(1, HALF)
+        interleave(2, 0)
+        for i in range(PACK):
+            gather(2, i, HALF)
+        interleave(2, HALF)
+        quantize(2, 0)
+        drain(0)
+        drain(1)
+        for i in range(PACK):
+            gather(2, i, HALF + QUARTER)
+        interleave(2, HALF + QUARTER)
+        quantize(2, HALF)
+        drain(2)
+        quantize(2, HALF + QUARTER)
+        drain(3)
+        scatter(0)
+        scatter(1)
+        nc.sync.dma_start(out, placed[:])

@@ -48,43 +48,46 @@ def tile_list_hboth_none_kernel(
         r8_s = keep.tile([P, PASSES, M], U8, name="r8_s", align_bytes=64)
         placed = keep.tile([P, T], F32, name="placed")
 
+        nc.vector.memset(r8_s[:].rearrange("p a n -> p (a n)").bitcast(I32), 0)
+        nc.vector.memset(w4_s[:].rearrange("p a n -> p (a n)").bitcast(I32), 0)
+        nc.vector.memset(placed[:], 0.0)
+
+        def load_plane(a, i):
+            nc.sync.dma_start(x[a][i][:], planes[a, i])
+
+        def load_scales(queue, scales, rows, q):
+            queue.dma_start(
+                scales[32 * q : 32 * q + 4].bitcast(I32),
+                rows[:, 4 * q : 4 * q + 4, :].rearrange("a r n -> r a n").bitcast(I32),
+            )
+
+        load_plane(0, 0)
         nc.sync.dma_start(gather_list[:], offs)
-        nc.sync.dma_start(x[0][0][:], planes[0, 0])
         nc.sync.dma_start(wgt_sb[0][:], wgt[:, 0:HALF])
         nc.sync.dma_start(wgt_sb[1][:], wgt[:, HALF:S])
         for i in range(1, PACK):
-            nc.sync.dma_start(x[0][i][:], planes[0, i])
-        nc.sync.dma_start(x[1][0][:], planes[1, 0])
+            load_plane(0, i)
+        for i in range(PACK):
+            load_plane(1, i)
+        load_plane(2, 0)
         nc.sync.dma_start(w4[:].bitcast(I32), w4_words.rearrange("a p b -> p a b").bitcast(I32))
         nc.sync.dma_start(r8[:].bitcast(I32), r8_words.rearrange("a p n i -> p a (n i)").bitcast(I32))
         for i in range(1, PACK):
-            nc.sync.dma_start(x[1][i][:], planes[1, i])
-        for i in range(PACK):
-            nc.sync.dma_start(x[2][i][:], planes[2, i])
+            load_plane(2, i)
+        for q in range(4):
+            load_scales(nc.sync, w4_s, w4_scales, q)
         nc.sync.dma_start(scatter_list[:], offs2)
         nc.sync.dma_start(wgo_sb[:], wgo)
-
-        nc.vector.memset(w4_s[:].rearrange("p a n -> p (a n)").bitcast(I32), 0)
-        nc.vector.memset(r8_s[:].rearrange("p a n -> p (a n)").bitcast(I32), 0)
-        nc.vector.memset(placed[:], 0.0)
-        for scales, rows in ((w4_s, w4_scales), (r8_s, r8_scales)):
-            for q in range(4):
-                nc.gpsimd.dma_start(
-                    scales[32 * q : 32 * q + 4].bitcast(I32),
-                    rows[:, 4 * q : 4 * q + 4, :].rearrange("a r n -> r a n").bitcast(I32),
-                )
+        for q in range(4):
+            load_scales(nc.gpsimd, r8_s, r8_scales, q)
 
         sums = [psum.tile([P, QUARTER], F32, name=f"sum{q}") for q in range(4)]
         y = [keep.tile([P, HALF], F32, name=f"y{h}") for h in range(2)]
 
-        chunks = [
-            [(0, HALF), (HALF, HALF)],
-            [(0, HALF), (HALF, HALF)],
-            [(0, HALF), (HALF, QUARTER), (HALF + QUARTER, QUARTER)],
-        ]
         state = {}
         for a in range(PASSES):
-            for j0, n in chunks[a]:
+            for j0 in (0, HALF):
+                n = HALF
                 state[a, j0] = (
                     n,
                     keep.tile([P, PACK, n], F32, name=f"g{a}_{j0}"),
@@ -103,9 +106,12 @@ def tile_list_hboth_none_kernel(
                 MULT,
             )
 
-        def interleave(a, j0):
+        def interleave(copy, a, j0, cols):
             n, g, b = state[a, j0][0:3]
-            nc.scalar.copy(b[:], g[:].rearrange("p i c -> p c i"))
+            copy(
+                b[:, cols, :].rearrange("p (c r) i -> p c i r", r=4),
+                g[:, :, cols].rearrange("p i (c r) -> p c i r", r=4),
+            )
 
         def quantize(a, j0):
             n, g, b, c, s = state[a, j0]
@@ -146,38 +152,26 @@ def tile_list_hboth_none_kernel(
                 MULT,
             )
 
-        for a in range(2):
+        whole, first, second = slice(0, HALF), slice(0, QUARTER), slice(QUARTER, HALF)
+        for a in range(PASSES):
             for i in range(PACK):
-                gather(a, i, 0)
-                if i == PACK - 1:
-                    interleave(a, 0)
-                gather(a, i, HALF)
-                if i == PACK - 1:
-                    interleave(a, HALF)
-                if a == 1 and i == 1:
-                    quantize(0, 0)
+                for j0 in (0, HALF):
+                    gather(a, i, j0)
+                    if i == PACK - 1 and a < PASSES - 1:
+                        interleave(nc.scalar.copy, a, j0, whole)
+                    if i == PACK - 1 and a == PASSES - 1:
+                        interleave(nc.scalar.copy, a, j0, first)
+                if a > 0 and i == 1:
+                    quantize(a - 1, 0)
                 if a == 1 and i == 2:
-                    quantize(0, HALF)
-        for i in range(PACK):
-            gather(2, i, 0)
-            if i == 1:
-                quantize(1, 0)
-            if i == 2:
-                quantize(1, HALF)
-        interleave(2, 0)
-        for i in range(PACK):
-            gather(2, i, HALF)
-        interleave(2, HALF)
+                    quantize(a - 1, HALF)
+        interleave(nc.vector.tensor_copy, 2, 0, second)
+        interleave(nc.vector.tensor_copy, 2, HALF, second)
         quantize(2, 0)
-        drain(0)
-        drain(1)
-        for i in range(PACK):
-            gather(2, i, HALF + QUARTER)
-        interleave(2, HALF + QUARTER)
+        quantize(1, HALF)
         quantize(2, HALF)
-        drain(2)
-        quantize(2, HALF + QUARTER)
-        drain(3)
+        for q in range(4):
+            drain(q)
         scatter(0)
         scatter(1)
         nc.sync.dma_start(out, placed[:])

@@ -48,8 +48,8 @@ def tile_list_hboth_none_kernel(
         r8_s = keep.tile([P, PASSES, M], U8, name="r8_s", align_bytes=64)
         placed = keep.tile([P, T], F32, name="placed")
 
-        nc.vector.memset(r8_s[:].rearrange("p a n -> p (a n)").bitcast(I32), 0)
         nc.vector.memset(w4_s[:].rearrange("p a n -> p (a n)").bitcast(I32), 0)
+        nc.vector.memset(r8_s[:].rearrange("p a n -> p (a n)").bitcast(I32), 0)
         nc.vector.memset(placed[:], 0.0)
 
         def load_plane(a, i):
@@ -65,21 +65,18 @@ def tile_list_hboth_none_kernel(
         nc.sync.dma_start(gather_list[:], offs)
         nc.sync.dma_start(wgt_sb[0][:], wgt[:, 0:HALF])
         nc.sync.dma_start(wgt_sb[1][:], wgt[:, HALF:S])
-        for i in range(1, PACK):
-            load_plane(0, i)
-        for i in range(PACK):
-            load_plane(1, i)
-        load_plane(2, 0)
-        nc.sync.dma_start(w4[:].bitcast(I32), w4_words.rearrange("a p b -> p a b").bitcast(I32))
+        for a in range(PASSES):
+            for i in range(PACK):
+                if (a, i) == (2, 1):
+                    nc.sync.dma_start(w4[:].bitcast(I32), w4_words.rearrange("a p b -> p a b").bitcast(I32))
+                if (a, i) != (0, 0):
+                    load_plane(a, i)
         nc.sync.dma_start(r8[:].bitcast(I32), r8_words.rearrange("a p n i -> p a (n i)").bitcast(I32))
-        for i in range(1, PACK):
-            load_plane(2, i)
         for q in range(4):
-            load_scales(nc.sync, w4_s, w4_scales, q)
+            load_scales(nc.gpsimd, w4_s, w4_scales, q)
+            load_scales(nc.sync, r8_s, r8_scales, q)
         nc.sync.dma_start(scatter_list[:], offs2)
         nc.sync.dma_start(wgo_sb[:], wgo)
-        for q in range(4):
-            load_scales(nc.gpsimd, r8_s, r8_scales, q)
 
         sums = [psum.tile([P, QUARTER], F32, name=f"sum{q}") for q in range(4)]
         y = [keep.tile([P, HALF], F32, name=f"y{h}") for h in range(2)]
@@ -118,27 +115,20 @@ def tile_list_hboth_none_kernel(
             nc.vector.quantize_mx(
                 out=c[:].bitcast(FP8X4), scales=s[:], in_=b[:].rearrange("p c i -> p (c i)")
             )
-            for k0 in range(0, n, QUARTER):
-                cols = slice(k0, k0 + QUARTER)
-                acc = sums[(j0 + k0) // QUARTER]
-                nc.tensor.matmul_mx(
-                    out=acc[:],
-                    lhsT=w4[:, a, :].bitcast(FP4X4),
-                    lhsT_scale=w4_s[:, a, :],
-                    rhs=c[:, cols].bitcast(FP8X4),
-                    rhs_scale=s[:, cols],
-                    start=(a == 0),
-                    stop=False,
-                )
-                nc.tensor.matmul_mx(
-                    out=acc[:],
-                    lhsT=r8[:, a, :].bitcast(FP8X4),
-                    lhsT_scale=r8_s[:, a, :],
-                    rhs=c[:, cols].bitcast(FP8X4),
-                    rhs_scale=s[:, cols],
-                    start=False,
-                    stop=(a == PASSES - 1),
-                )
+
+        def multiply(a, q, kind):
+            c, s = state[a, q // 2 * HALF][3:5]
+            cols = slice(q % 2 * QUARTER, (q % 2 + 1) * QUARTER)
+            words, dtype, scales = (w4, FP4X4, w4_s) if kind == 4 else (r8, FP8X4, r8_s)
+            nc.tensor.matmul_mx(
+                out=sums[q][:],
+                lhsT=words[:, a, :].bitcast(dtype),
+                lhsT_scale=scales[:, a, :],
+                rhs=c[:, cols].bitcast(FP8X4),
+                rhs_scale=s[:, cols],
+                start=(a == 0 and kind == 4),
+                stop=(a == PASSES - 1 and kind == 8),
+            )
 
         def drain(q):
             c0 = (q % 2) * QUARTER
@@ -153,6 +143,12 @@ def tile_list_hboth_none_kernel(
             )
 
         whole, first, second = slice(0, HALF), slice(0, QUARTER), slice(QUARTER, HALF)
+
+        def quantize_early(a, j0):
+            quantize(a, j0)
+            for q in (j0 // QUARTER, j0 // QUARTER + 1):
+                multiply(a, q, 4)
+
         for a in range(PASSES):
             for i in range(PACK):
                 for j0 in (0, HALF):
@@ -162,14 +158,26 @@ def tile_list_hboth_none_kernel(
                     if i == PACK - 1 and a == PASSES - 1:
                         interleave(nc.scalar.copy, a, j0, first)
                 if a > 0 and i == 1:
-                    quantize(a - 1, 0)
+                    quantize_early(a - 1, 0)
                 if a == 1 and i == 2:
-                    quantize(a - 1, HALF)
+                    quantize_early(a - 1, HALF)
+        for q in (0, 1):
+            multiply(0, q, 8)
+            multiply(1, q, 8)
         interleave(nc.vector.tensor_copy, 2, 0, second)
         interleave(nc.vector.tensor_copy, 2, HALF, second)
         quantize(2, 0)
-        quantize(1, HALF)
+        for q in (0, 1):
+            multiply(2, q, 4)
+            multiply(2, q, 8)
+        quantize_early(1, HALF)
+        for q in (2, 3):
+            multiply(0, q, 8)
+            multiply(1, q, 8)
         quantize(2, HALF)
+        for q in (2, 3):
+            multiply(2, q, 4)
+            multiply(2, q, 8)
         for q in range(4):
             drain(q)
         scatter(0)

from contextlib import ExitStack

import concourse.mybir as mybir

K, M, T, S = 1536, 128, 1024, 512
FLOPS = 2 * 2 * K * M * S

P = 128
PACK = 4
PASSES = K // (P * PACK)
HALF = S // 2
QUARTER = S // 4
LANES = 16

F32 = mybir.dt.float32
BF16 = mybir.dt.bfloat16
I32 = mybir.dt.int32
U32 = mybir.dt.uint32
U16 = mybir.dt.uint16
U8 = mybir.dt.uint8
FP8X4 = mybir.dt.float8_e4m3fn_x4
FP4X4 = mybir.dt.float4_e2m1fn_x4
MULT = mybir.AluOpType.mult


def tile_list_hboth_none_kernel(
    tc, xT, w4_words, w4_scales, r8_words, r8_scales, wgt, wgo, offs, offs2, out
):
    nc = tc.nc
    with ExitStack() as ctx:
        lists = ctx.enter_context(tc.tile_pool(name="lists", bufs=1))
        keep = ctx.enter_context(tc.tile_pool(name="keep", bufs=1))
        psum = ctx.enter_context(tc.psum_pool(name="psum", bufs=1))

        gather_list = lists.tile([P, S // LANES], U16, name="gather_list")
        scatter_list = lists.tile([P, S // LANES], U16, name="scatter_list")

        planes = xT.rearrange("(a p i) t -> a i p t", a=PASSES, i=PACK)
        x = [
            [keep.tile([P, T], F32, name=f"x{a}_{i}") for i in range(PACK)]
            for a in range(PASSES)
        ]
        wgt_sb = [keep.tile([P, HALF], F32, name=f"wgt{h}") for h in range(2)]
        wgo_sb = keep.tile([P, S], F32, name="wgo_sb")
        w4 = keep.tile([P, PASSES, 2 * M], U8, name="w4", align_bytes=64)
        r8 = keep.tile([P, PASSES, PACK * M], U8, name="r8", align_bytes=64)
        w4_s = keep.tile([P, PASSES, M], U8, name="w4_s", align_bytes=64)
        r8_s = keep.tile([P, PASSES, M], U8, name="r8_s", align_bytes=64)
        placed = keep.tile([P, T], F32, name="placed")

        nc.vector.memset(w4_s[:].rearrange("p a n -> p (a n)").bitcast(I32), 0)
        nc.vector.memset(r8_s[:].rearrange("p a n -> p (a n)").bitcast(I32), 0)
        nc.vector.memset(placed[:], 0.0)

        def load_plane(a, i):
            nc.sync.dma_start(x[a][i][:], planes[a, i])

        def load_scales(queue, scales, rows, q):
            queue.dma_start(
                scales[32 * q : 32 * q + 4].bitcast(I32),
                rows[:, 4 * q : 4 * q + 4, :].rearrange("a r n -> r a n").bitcast(I32),
            )

        load_plane(0, 0)
        nc.sync.dma_start(gather_list[:], offs)
        nc.sync.dma_start(wgt_sb[0][:], wgt[:, 0:HALF])
        nc.sync.dma_start(wgt_sb[1][:], wgt[:, HALF:S])
        for a in range(PASSES):
            for i in range(PACK):
                if (a, i) == (2, 1):
                    nc.sync.dma_start(w4[:].bitcast(I32), w4_words.rearrange("a p b -> p a b").bitcast(I32))
                if (a, i) != (0, 0):
                    load_plane(a, i)
        nc.sync.dma_start(r8[:].bitcast(I32), r8_words.rearrange("a p n i -> p a (n i)").bitcast(I32))
        for q in range(4):
            load_scales(nc.gpsimd, w4_s, w4_scales, q)
            load_scales(nc.sync, r8_s, r8_scales, q)
        nc.sync.dma_start(scatter_list[:], offs2)
        nc.sync.dma_start(wgo_sb[:], wgo)

        sums = [psum.tile([P, QUARTER], F32, name=f"sum{q}") for q in range(4)]
        y = [keep.tile([P, HALF], F32, name=f"y{h}") for h in range(2)]

        state = {}
        for a in range(PASSES):
            for j0 in (0, HALF):
                n = HALF
                state[a, j0] = (
                    n,
                    keep.tile([P, PACK, n], F32, name=f"g{a}_{j0}"),
                    keep.tile([P, n, PACK], BF16, name=f"b{a}_{j0}", align_bytes=64),
                    keep.tile([P, n], U32, name=f"c{a}_{j0}", align_bytes=64),
                    keep.tile([P, n], U8, name=f"s{a}_{j0}", align_bytes=64),
                )

        def gather(a, i, j0):
            n, g = state[a, j0][0:2]
            w0 = j0 % HALF
            nc.vector.tensor_tensor(
                g[:, i, :],
                x[a][i][:].indirect(gather_list[:, j0 // LANES : (j0 + n) // LANES]),
                wgt_sb[j0 // HALF][:, w0 : w0 + n],
                MULT,
            )

        def interleave(copy, a, j0, cols):
            n, g, b = state[a, j0][0:3]
            copy(
                b[:, cols, :].rearrange("p (c r) i -> p c i r", r=4),
                g[:, :, cols].rearrange("p i (c r) -> p c i r", r=4),
            )

        def quantize(a, j0):
            n, g, b, c, s = state[a, j0]
            nc.vector.quantize_mx(
                out=c[:].bitcast(FP8X4), scales=s[:], in_=b[:].rearrange("p c i -> p (c i)")
            )

        def multiply(a, q, kind):
            c, s = state[a, q // 2 * HALF][3:5]
            cols = slice(q % 2 * QUARTER, (q % 2 + 1) * QUARTER)
            words, dtype, scales = (w4, FP4X4, w4_s) if kind == 4 else (r8, FP8X4, r8_s)
            nc.tensor.matmul_mx(
                out=sums[q][:],
                lhsT=words[:, a, :].bitcast(dtype),
                lhsT_scale=scales[:, a, :],
                rhs=c[:, cols].bitcast(FP8X4),
                rhs_scale=s[:, cols],
                start=(a == 0 and kind == 4),
                stop=(a == PASSES - 1 and kind == 8),
            )

        def drain(q):
            c0 = (q % 2) * QUARTER
            nc.scalar.copy(y[q // 2][:, c0 : c0 + QUARTER], sums[q][:])

        def scatter(h):
            nc.vector.tensor_tensor(
                placed[:].indirect(scatter_list[:, h * HALF // LANES : (h + 1) * HALF // LANES]),
                y[h][:],
                wgo_sb[:, h * HALF : (h + 1) * HALF],
                MULT,
            )

        whole, first, second = slice(0, HALF), slice(0, QUARTER), slice(QUARTER, HALF)

        def quantize_early(a, j0):
            quantize(a, j0)
            for q in (j0 // QUARTER, j0 // QUARTER + 1):
                multiply(a, q, 4)

        for a in range(PASSES):
            for i in range(PACK):
                for j0 in (0, HALF):
                    gather(a, i, j0)
                    if i == PACK - 1 and a < PASSES - 1:
                        interleave(nc.scalar.copy, a, j0, whole)
                    if i == PACK - 1 and a == PASSES - 1:
                        interleave(nc.scalar.copy, a, j0, first)
                if a > 0 and i == 1:
                    quantize_early(a - 1, 0)
                if a == 1 and i == 2:
                    quantize_early(a - 1, HALF)
        for q in (0, 1):
            multiply(0, q, 8)
            multiply(1, q, 8)
        interleave(nc.vector.tensor_copy, 2, 0, second)
        interleave(nc.vector.tensor_copy, 2, HALF, second)
        quantize(2, 0)
        for q in (0, 1):
            multiply(2, q, 4)
            multiply(2, q, 8)
        quantize_early(1, HALF)
        for q in (2, 3):
            multiply(0, q, 8)
            multiply(1, q, 8)
        quantize(2, HALF)
        for q in (2, 3):
            multiply(2, q, 4)
            multiply(2, q, 8)
        for q in range(4):
            drain(q)
        scatter(0)
        scatter(1)
        nc.sync.dma_start(out, placed[:])
